import numpy as np
import ml_dtypes


def mxq(x, axis, fmt="e4m3"):
    dtype, down = {"e4m3": (ml_dtypes.float8_e4m3fn, 7), "e5m2": (ml_dtypes.float8_e5m2, 14)}[fmt]
    v = np.moveaxis(np.asarray(x, np.float32).astype(ml_dtypes.bfloat16).astype(np.float64), axis, -1)
    blocks = v.reshape(v.shape[:-1] + (-1, 32))
    amax = np.abs(blocks).max(-1, keepdims=True)
    byte = np.maximum(np.where(amax > 0, np.frexp(amax)[1] - 1 + 127, 0) - down, 1)
    scale = np.exp2(byte - 127.0)
    codes = (blocks / scale).astype(np.float32).astype(dtype).astype(np.float64)
    return np.moveaxis((codes * scale).reshape(v.shape), -1, axis)


WIDE = False


def mx_kscale(k):
    if not WIDE:
        return np.ones(k)
    levels = np.array([10, -10, 5, -5, 0])
    if k % 512:
        return np.exp2(np.random.permutation(np.resize(levels, k // 32))).repeat(32)
    a = np.empty((k // 512, 16))
    for p in range(k // 512):
        a[p, :8] = np.random.permutation(np.resize(levels, 8))
        for g in range(8):
            far = levels[np.abs(levels - a[p, g]) >= 10]
            a[p, g + 8] = far[np.random.randint(len(far))]
    return np.exp2(a.ravel()).repeat(32)


def f64(x):
    return np.asarray(x).astype(np.float64)


def striped(idx):
    return np.tile(idx.reshape(-1, 16).T, (8, 1)).astype(np.uint16)


def unstriped(offs):
    return offs[:16].T.reshape(-1).astype(np.int64)


E2M1 = np.array([0.0, 0.5, 1.0, 1.5, 2.0, 3.0, 4.0, 6.0, -0.0, -0.5, -1.0, -1.5, -2.0, -3.0, -4.0, -6.0])


def pack_weight(w, fmt):
    k, n = w.shape
    w = f64(np.asarray(w, np.float32).astype(ml_dtypes.bfloat16)).reshape(k // 32, 32, n)
    amax = np.abs(w).max(1)
    if fmt == "e4m3":
        byte = np.frexp(amax)[1] - 1 + 127 - 7
    else:
        mant, ex = np.frexp(amax / 6.0)
        byte = np.where(mant > 0.5, ex, ex - 1) + 127
    byte = np.clip(np.where(amax > 0, byte, 1), 1, 254)
    scaled = (w * np.exp2(127.0 - byte)[:, None, :]).reshape(k, n).astype(np.float32)
    by_word = np.ascontiguousarray(scaled.reshape(k // 512, 128, 4, n).transpose(0, 1, 3, 2))
    if fmt == "e4m3":
        words = by_word.astype(ml_dtypes.float8_e4m3fn).view(np.uint8)
    else:
        c = by_word.astype(ml_dtypes.float4_e2m1fn).view(np.uint8) & 0xF
        words = (c[..., 0::2] | (c[..., 1::2] << 4)).reshape(k // 512, 128, 2 * n)
    return np.ascontiguousarray(words), np.ascontiguousarray(byte.astype(np.uint8).reshape(k // 512, 16, n))


def unpack_weight(words, scales, fmt):
    g, _, n = scales.shape
    words = np.ascontiguousarray(words).reshape(g, 128, n, -1)
    if fmt == "e4m3":
        vals = words.view(ml_dtypes.float8_e4m3fn).astype(np.float64)
    else:
        nib = np.empty((g, 128, n, 4), np.uint8)
        nib[..., 0::2] = words & 0xF
        nib[..., 1::2] = words >> 4
        vals = E2M1[nib]
    vals = vals * np.repeat(np.exp2(scales.astype(np.float64) - 127.0), 8, axis=1)[..., None]
    return vals.transpose(0, 1, 3, 2).reshape(g * 512, n)


def gelu(v):
    return 0.5 * v * (1.0 + np.tanh(np.sqrt(2.0 / np.pi) * (v + 0.044715 * v**3)))


K, H, T, S, T2, P, T3, S2 = 1536, 1024, 2048, 512, 1024, 512, 2048, 1024

def setup_inputs():
    n = np.random.standard_normal
    s = mx_kscale(K)[:, None]
    u = mx_kscale(H)[:, None]
    tab_words, tab_scales = pack_weight(n((K, T)) * s, "e4m3")
    tab2_words, tab2_scales = pack_weight(n((H, T3)) / np.sqrt(H) / u, "e4m3")
    w4_words, w4_scales = pack_weight(0.8 * n((K, H)) / np.sqrt(K) / s, "e2m1")
    return {
        "tab_words": tab_words, "tab_scales": tab_scales,
        "tab2_words": tab2_words, "tab2_scales": tab2_scales,
        "w4_words": w4_words, "w4_scales": w4_scales,
        "w1": (1.3 * n((K, H)) / np.sqrt(K) / s).astype(np.float32),
        "b1": (0.7 * n(H)).astype(np.float32),
        "gain": (np.exp(0.3 * n(H)) * u[:, 0]).astype(np.float32),
        "page0": (n((H, T2)) * u).astype(np.float32),
        "wgs": np.exp(0.3 * n((128, S))).astype(np.float32),
        "comp": (1.0 + 0.5 * n((H, P))).astype(np.float32),
        "link": n((S2, P)).astype(np.float32),
        "offs": striped(np.random.permutation(T)[:S]),
        "offs2": striped(np.random.permutation(T3)[:S2]),
        "offs3": striped(np.random.permutation(T2)[:S]),
        "offs4": striped(np.random.permutation(T2)[:P]),
    }

def reference(tab_words, tab_scales, tab2_words, tab2_scales, w4_words, w4_scales, w1, b1, gain, page0, wgs, comp, link, offs, offs2, offs3, offs4):
    v = unpack_weight(tab_words, tab_scales, "e4m3")[:, unstriped(offs)]
    v2 = unpack_weight(tab2_words, tab2_scales, "e4m3")[:, unstriped(offs2)]
    w4 = unpack_weight(w4_words, w4_scales, "e2m1")
    bent = np.tanh((mxq(f64(w1), 0, "e4m3").T @ v) + f64(b1)[:, None])
    h = f64(gain)[:, None] * (bent + (w4.T @ v))
    page = f64(page0).copy()
    page[:, unstriped(offs3)] = np.tile(f64(wgs), (H // 128, 1)) * h
    x = f64(comp) * page[:, unstriped(offs4)]
    e = v2.T @ mxq(x, 0, "e4m3")
    return np.maximum(e, f64(link))

@@ -1,0 +1,322 @@
+from contextlib import ExitStack
+
+import concourse.mybir as mybir
+
+K, H, T, S, T2, P_SLOTS, T3, S2 = 1536, 1024, 2048, 512, 1024, 512, 2048, 1024
+FLOPS = 2 * (2 * K * H * S + H * S2 * P_SLOTS)
+
+F32 = mybir.dt.float32
+BF16 = mybir.dt.bfloat16
+I32 = mybir.dt.int32
+U32 = mybir.dt.uint32
+U16 = mybir.dt.uint16
+U8 = mybir.dt.uint8
+FP8X4 = mybir.dt.float8_e4m3fn_x4
+FP4X4 = mybir.dt.float4_e2m1fn_x4
+ALU = mybir.AluOpType
+ACT = mybir.ActivationFunctionType
+
+P = 128
+PACK = 4
+PASS = P * PACK
+KP = K // PASS
+HP = H // PASS
+QUADS = 4
+SHIFT_ROWS = 100
+
+
+def tile_list_duplicate_report_finder_kernel(
+    tc, tab_words, tab_scales, tab2_words, tab2_scales, w4_words, w4_scales, w1, b1, gain,
+    page0, wgs, comp, link, offs, offs2, offs3, offs4, out,
+):
+    nc = tc.nc
+    with ExitStack() as ctx:
+        lists = ctx.enter_context(tc.tile_pool(name="lists", bufs=1))
+        keep = ctx.enter_context(tc.tile_pool(name="keep", bufs=1))
+        psum = ctx.enter_context(tc.psum_pool(name="psum", bufs=1))
+
+        def held(shape, dtype, name, tag=None, bufs=1):
+            return keep.tile(shape, dtype, name=name, tag=tag or name, bufs=bufs, align_bytes=64)
+
+        def bank(i, name):
+            return psum.tile([P, 512], F32, name=name, tag="bank%d" % i)
+
+        idx = lists.tile([P, S // 16], U16, name="idx")
+        idx2 = lists.tile([P, S2 // 16], U16, name="idx2")
+        idx3 = lists.tile([P, S // 16], U16, name="idx3")
+        idx4 = lists.tile([P, P_SLOTS // 16], U16, name="idx4")
+
+        tab_sc = held([P, T], U8, "tab_sc")
+        w4_sc_raw = held([P, KP, H], U8, "w4_sc_raw")
+        tab2_sc = held([P, T3], U8, "tab2_sc")
+        v_sc_low = [held([P, S], U8, "v_sc_low%d" % a) for a in range(1, KP)]
+        nc.vector.memset(tab_sc[:].bitcast(I32), 0)
+        nc.vector.memset(w4_sc_raw[:].bitcast(I32), 0)
+        nc.vector.memset(tab2_sc[:].bitcast(I32), 0)
+        for plane in v_sc_low:
+            nc.vector.memset(plane[:].bitcast(I32), 0)
+        for q in range(QUADS):
+            nc.gpsimd.dma_start(
+                out=tab_sc[32 * q : 32 * q + 4 * KP, :].bitcast(I32),
+                in_=tab_scales[:, 4 * q : 4 * q + 4, :].bitcast(I32),
+            )
+        for q in range(QUADS):
+            nc.gpsimd.dma_start(
+                out=tab2_sc[32 * q + 8 : 32 * q + 8 + 4 * HP, :].bitcast(I32),
+                in_=tab2_scales[:, 4 * q : 4 * q + 4, :].bitcast(I32),
+            )
+
+        def load_w1(a, b):
+            raw = held([P, PACK, PASS], F32, "w1_raw%d%d" % (a, b), tag="rows", bufs=4)
+            rows = w1[PASS * a : PASS * (a + 1), PASS * b : PASS * (b + 1)]
+            nc.sync.dma_start(out=raw[:], in_=rows.rearrange("(p j) c -> p j c", j=PACK))
+            return raw
+
+        def load_words(words, a, name):
+            tile = held([P, T], I32, name, tag="table", bufs=3)
+            nc.sync.dma_start(out=tile[:], in_=words[a].rearrange("p t i -> p (t i)").bitcast(I32))
+            return tile
+
+        page_rows = page0.rearrange("(b p t) c -> b t p c", p=P, t=PACK)
+
+        def load_page(s):
+            tile = held([P, T2], F32, "page%d" % s)
+            nc.sync.dma_start(out=tile[:], in_=page_rows[s // PACK, s % PACK])
+            return tile
+
+        comp_rows = comp.rearrange("(b p t) j -> b p t j", p=P, t=PACK)
+
+        def load_comp(pair):
+            tile = held([P, 2, P_SLOTS], F32, "comp%d" % pair)
+            b, t0 = pair // 2, 2 * (pair % 2)
+            nc.sync.dma_start(out=tile[:], in_=comp_rows[b, :, t0 : t0 + 2, :])
+            return tile
+
+        wgs_rows = wgs.rearrange("(q t) j -> q t j", t=PACK)
+
+        def load_wgs(t0, t1, name):
+            tile = held([P, t1 - t0, S], F32, name)
+            for q in range(QUADS):
+                nc.sync.dma_start(out=tile[32 * q : 32 * (q + 1)], in_=wgs_rows[:, t0:t1, :])
+            return tile
+
+        def load_link(half):
+            tile = held([P, 4, P_SLOTS], F32, "link%d" % half, tag="rows", bufs=4)
+            rows = link[512 * half : 512 * (half + 1), :]
+            nc.sync.dma_start(out=tile[:], in_=rows.rearrange("(i p) j -> p i j", p=P))
+            return tile
+
+        w1_raw, tab_w, tab2_w, pages, comps = {}, {}, {}, {}, {}
+        nc.sync.dma_start(idx[:], offs)
+        w1_raw[0, 0] = load_w1(0, 0)
+        for q in range(QUADS):
+            nc.sync.dma_start(
+                out=w4_sc_raw[32 * q : 32 * q + 4].bitcast(I32),
+                in_=w4_scales[:, 4 * q : 4 * q + 4, :].rearrange("a r c -> r a c").bitcast(I32),
+            )
+        w1_raw[1, 0] = load_w1(1, 0)
+        w4_raw = held([P, KP, 2 * H], U8, "w4_raw")
+        nc.sync.dma_start(out=w4_raw[:].bitcast(I32), in_=w4_words.rearrange("a p c -> p a c").bitcast(I32))
+        w1_raw[2, 0] = load_w1(2, 0)
+        b1_sb = held([P, HP, PACK], F32, "b1_sb")
+        gain_sb = held([P, HP, PACK], F32, "gain_sb")
+        nc.sync.dma_start(out=b1_sb[:], in_=b1.rearrange("(b p t) -> p b t", p=P, t=PACK))
+        nc.sync.dma_start(out=gain_sb[:], in_=gain.rearrange("(b p t) -> p b t", p=P, t=PACK))
+        nc.sync.dma_start(idx2[:], offs2)
+        tab_w[0] = load_words(tab_words, 0, "tab_w0")
+        nc.sync.dma_start(idx3[:], offs3)
+        tab_w[1] = load_words(tab_words, 1, "tab_w1")
+        nc.sync.dma_start(idx4[:], offs4)
+        tab_w[2] = load_words(tab_words, 2, "tab_w2")
+        wgs_first = load_wgs(0, 1, "wgs_first")
+        pages[0] = load_page(0)
+        comps[0] = load_comp(0)
+        wgs_rest = load_wgs(1, PACK, "wgs_rest")
+        pages[1] = load_page(1)
+        w1_raw[0, 1] = load_w1(0, 1)
+        pages[2] = load_page(2)
+        comps[1] = load_comp(1)
+
+        v_sc = held([P, S], U8, "v_sc")
+        nc.vector.tensor_copy(out=v_sc[:], in_=tab_sc[:].indirect(idx[:]))
+        for a in range(1, KP):
+            nc.gpsimd.dma_start(
+                out=v_sc_low[a - 1][0:SHIFT_ROWS, :].bitcast(I32),
+                in_=v_sc[4 * a : 4 * a + SHIFT_ROWS, :].bitcast(I32),
+            )
+        v_sc_at0 = [v_sc] + v_sc_low
+
+        w4_sc = held([P, KP * H], U8, "w4_sc")
+        nc.vector.tensor_copy(
+            out=w4_sc[:].rearrange("p (g t m) -> p g t m", t=PACK, m=P),
+            in_=w4_sc_raw[:].rearrange("p a (b m t) -> p (a b) t m", t=PACK, m=P),
+        )
+        w4_w = held([P, KP * 2 * H], U8, "w4_w")
+        nc.vector.tensor_copy(
+            out=w4_w[:].bitcast(U16).rearrange("p (g t m) -> p g t m", t=PACK, m=P),
+            in_=w4_raw[:].bitcast(U16).rearrange("p a (b m t) -> p (a b) t m", t=PACK, m=P),
+        )
+
+        w1_w, w1_sc = {}, {}
+
+        def quantize_w1(a, b):
+            rounded = held([P, PACK * PASS], BF16, "w1_bf%d%d" % (a, b), tag="w1_bf", bufs=3)
+            nc.scalar.copy(
+                out=rounded[:].rearrange("p (t m j) -> p m j t", t=PACK, j=PACK),
+                in_=w1_raw[a, b][:].rearrange("p j (m t) -> p m j t", t=PACK),
+            )
+            w1_w[a, b] = held([P, PASS], U32, "w1_w%d%d" % (a, b))
+            w1_sc[a, b] = held([P, PASS], U8, "w1_sc%d%d" % (a, b))
+            nc.vector.quantize_mx(out=w1_w[a, b][:].bitcast(FP8X4), scales=w1_sc[a, b][:], in_=rounded[:])
+
+        for a in range(KP):
+            quantize_w1(a, 0)
+
+        w1_raw[1, 1] = load_w1(1, 1)
+        pages[3] = load_page(3)
+        w1_raw[2, 1] = load_w1(2, 1)
+        pages[4] = load_page(4)
+        comps[2] = load_comp(2)
+        pages[5] = load_page(5)
+
+        v_w = []
+        for a in range(KP):
+            words = held([P, S], U32, "v_w%d" % a)
+            nc.vector.tensor_copy(out=words[:], in_=tab_w[a][:].bitcast(U32).indirect(idx[:]))
+            v_w.append(words)
+
+        v2_sc = held([P, S2], U8, "v2_sc")
+        nc.vector.tensor_copy(out=v2_sc[:], in_=tab2_sc[:].indirect(idx2[:]))
+
+        tab2_w[0] = load_words(tab2_words, 0, "tab2_w0")
+        pages[6] = load_page(6)
+        comps[3] = load_comp(3)
+        pages[7] = load_page(7)
+        tab2_w[1] = load_words(tab2_words, 1, "tab2_w1")
+
+        def first_pass(s, a, acc1, acc4):
+            b, t = divmod(s, PACK)
+            nc.tensor.matmul_mx(
+                out=acc1[:],
+                lhsT=w1_w[a, b][:, P * t : P * (t + 1)].bitcast(FP8X4),
+                lhsT_scale=w1_sc[a, b][:, P * t : P * (t + 1)],
+                rhs=v_w[a][:].bitcast(FP8X4),
+                rhs_scale=v_sc[4 * a : P, :],
+                start=(a == 0), stop=(a == KP - 1),
+            )
+            c0 = H * a + P * s
+            nc.tensor.matmul_mx(
+                out=acc4[:],
+                lhsT=w4_w[:, 2 * c0 : 2 * (c0 + P)].bitcast(FP4X4),
+                lhsT_scale=w4_sc[:, c0 : c0 + P],
+                rhs=v_w[a][:].bitcast(FP8X4),
+                rhs_scale=v_sc_at0[a][:],
+                start=(a == 0), stop=(a == KP - 1),
+            )
+
+        accs = {}
+
+        def open_banks(s):
+            accs[s] = (bank(2 * (s % 4), "acc1_%d" % s), bank(2 * (s % 4) + 1, "acc4_%d" % s))
+
+        for s in range(PACK):
+            open_banks(s)
+        for a in range(KP):
+            for s in range(2):
+                first_pass(s, a, *accs[s])
+        for s in range(2, PACK):
+            for a in range(KP):
+                first_pass(s, a, *accs[s])
+
+        picked = [held([P, PACK, P_SLOTS], F32, "picked%d" % b) for b in range(HP)]
+        sums, weights = {}, {}
+
+        def features(s):
+            b, t = divmod(s, PACK)
+            acc1, acc4 = accs[s]
+            bent = held([P, S], F32, "bent%d" % s, tag="bent", bufs=4)
+            nc.scalar.activation(out=bent[:], in_=acc1[:], func=ACT.Tanh, bias=b1_sb[:, b, t : t + 1])
+            weights[s] = held([P, S], F32, "weight%d" % s, tag="weight", bufs=3)
+            rows = wgs_first[:, 0, :] if t == 0 else wgs_rest[:, t - 1, :]
+            nc.scalar.activation(out=weights[s][:], in_=rows, func=ACT.Copy, scale=gain_sb[:, b, t : t + 1])
+            sums[s] = held([P, S], F32, "sum%d" % s, tag="sum", bufs=3)
+            nc.vector.tensor_tensor(out=sums[s][:], in0=acc4[:], in1=bent[:], op=ALU.add)
+
+        def put(s):
+            nc.vector.tensor_tensor(pages[s][:].indirect(idx3[:]), sums[s][:], weights[s][:], ALU.mult)
+
+        def fetch(s):
+            b, t = divmod(s, PACK)
+            nc.vector.tensor_tensor(
+                picked[b][:, t, :], pages[s][:].indirect(idx4[:]), comps[s // 2][:, s % 2, :], ALU.mult
+            )
+
+        x_bf, x_w, x_sc = {}, {}, {}
+
+        def round_x(b):
+            x_bf[b] = held([P, PACK * P_SLOTS], BF16, "x_bf%d" % b)
+            nc.scalar.copy(
+                out=x_bf[b][:].rearrange("p (c i t) -> p c t i", i=4, t=PACK),
+                in_=picked[b][:].rearrange("p t (c i) -> p c t i", i=4),
+            )
+
+        def quantize_x(b):
+            x_w[b] = held([P, P_SLOTS], U32, "x_w%d" % b)
+            x_sc[b] = held([P, P_SLOTS], U8, "x_sc%d" % b)
+            nc.vector.quantize_mx(out=x_w[b][:].bitcast(FP8X4), scales=x_sc[b][:], in_=x_bf[b][:])
+
+        v2_w = {}
+
+        def gather_v2(a, half, words):
+            nc.vector.tensor_copy(
+                out=words, in_=tab2_w[a][:].bitcast(U32).indirect(idx2[:, 32 * half : 32 * (half + 1)])
+            )
+            v2_w[a, half] = words
+
+        links = {}
+        features(0)
+        for s in range(2 * PACK):
+            put(s)
+            if s < KP:
+                quantize_w1(s, 1)
+            if s == KP - 1:
+                links[0] = load_link(0)
+                links[1] = load_link(1)
+            if s + 1 < 2 * PACK:
+                if s + 1 >= PACK:
+                    open_banks(s + 1)
+                    for a in range(KP):
+                        first_pass(s + 1, a, *accs[s + 1])
+                features(s + 1)
+            fetch(s)
+            if s == PACK - 1:
+                round_x(0)
+            if s == PACK:
+                quantize_x(0)
+                first_words = held([P, 512], U32, "v2_first")
+                gather_v2(0, 0, first_words[:])
+
+        round_x(1)
+        late_words = held([P, 2, 512], U32, "v2_late", tag="page7")
+        gather_v2(1, 0, late_words[:, 0, :])
+        gather_v2(0, 1, late_words[:, 1, :])
+        quantize_x(1)
+        last_words = held([P, 512], U32, "v2_last", tag="x_bf1")
+        gather_v2(1, 1, last_words[:])
+
+        bank_order = [0, 2, 1, 3, 4, 6, 5, 7]
+        for i in range(S2 // P):
+            half, m0 = i // 4, P * (i % 4)
+            acc = bank(bank_order[i], "score%d" % i)
+            for a in range(HP):
+                nc.tensor.matmul_mx(
+                    out=acc[:],
+                    lhsT=v2_w[a, half][:, m0 : m0 + P].bitcast(FP8X4),
+                    lhsT_scale=v2_sc[8 + 4 * a : P, P * i : P * (i + 1)],
+                    rhs=x_w[a][:].bitcast(FP8X4),
+                    rhs_scale=x_sc[a][:],
+                    start=(a == 0), stop=(a == HP - 1),
+                )
+            floor = links[half][:, i % 4, :]
+            nc.vector.tensor_tensor(out=floor, in0=acc[:], in1=floor, op=ALU.max)
+            nc.sync.dma_start(out=out[P * i : P * (i + 1), :], in_=floor)

@@ -22,7 +22,6 @@ PASS = P * PACK
 KP = K // PASS
 HP = H // PASS
 QUADS = 4
-SHIFT_ROWS = 100
 
 
 def tile_list_duplicate_report_finder_kernel(
@@ -46,20 +45,13 @@ def tile_list_duplicate_report_finder_kernel(
         idx3 = lists.tile([P, S // 16], U16, name="idx3")
         idx4 = lists.tile([P, P_SLOTS // 16], U16, name="idx4")
 
-        tab_sc = held([P, T], U8, "tab_sc")
+        tab_sc = held([P, KP, T], U8, "tab_sc")
         w4_sc_raw = held([P, KP, H], U8, "w4_sc_raw")
         tab2_sc = held([P, T3], U8, "tab2_sc")
-        v_sc_low = [held([P, S], U8, "v_sc_low%d" % a) for a in range(1, KP)]
-        nc.vector.memset(tab_sc[:].bitcast(I32), 0)
+        nc.vector.memset(tab_sc[:, 0:2, :].bitcast(I32), 0)
+        nc.gpsimd.memset(tab_sc[:, 2, :].bitcast(I32), 0)
         nc.vector.memset(w4_sc_raw[:].bitcast(I32), 0)
-        nc.vector.memset(tab2_sc[:].bitcast(I32), 0)
-        for plane in v_sc_low:
-            nc.vector.memset(plane[:].bitcast(I32), 0)
-        for q in range(QUADS):
-            nc.gpsimd.dma_start(
-                out=tab_sc[32 * q : 32 * q + 4 * KP, :].bitcast(I32),
-                in_=tab_scales[:, 4 * q : 4 * q + 4, :].bitcast(I32),
-            )
+        nc.gpsimd.memset(tab2_sc[:].bitcast(I32), 0)
         for q in range(QUADS):
             nc.gpsimd.dma_start(
                 out=tab2_sc[32 * q + 8 : 32 * q + 8 + 4 * HP, :].bitcast(I32),
@@ -67,13 +59,13 @@ def tile_list_duplicate_report_finder_kernel(
             )
 
         def load_w1(a, b):
-            raw = held([P, PACK, PASS], F32, "w1_raw%d%d" % (a, b), tag="rows", bufs=4)
+            raw = held([P, PACK, PASS], F32, "w1_raw%d%d" % (a, b))
             rows = w1[PASS * a : PASS * (a + 1), PASS * b : PASS * (b + 1)]
             nc.sync.dma_start(out=raw[:], in_=rows.rearrange("(p j) c -> p j c", j=PACK))
             return raw
 
         def load_words(words, a, name):
-            tile = held([P, T], I32, name, tag="table", bufs=3)
+            tile = held([P, T], I32, name, tag="table%d" % a)
             nc.sync.dma_start(out=tile[:], in_=words[a].rearrange("p t i -> p (t i)").bitcast(I32))
             return tile
 
@@ -101,50 +93,66 @@ def tile_list_duplicate_report_finder_kernel(
             return tile
 
         def load_link(half):
-            tile = held([P, 4, P_SLOTS], F32, "link%d" % half, tag="rows", bufs=4)
+            tile = held([P, 4, P_SLOTS], F32, "link%d" % half, tag="w1_raw%d1" % (half + 1))
             rows = link[512 * half : 512 * (half + 1), :]
             nc.sync.dma_start(out=tile[:], in_=rows.rearrange("(i p) j -> p i j", p=P))
             return tile
 
         w1_raw, tab_w, tab2_w, pages, comps = {}, {}, {}, {}, {}
-        nc.sync.dma_start(idx[:], offs)
-        w1_raw[0, 0] = load_w1(0, 0)
-        for q in range(QUADS):
+        w4_raw = held([P, KP, 2 * H], U8, "w4_raw")
+        b1_sb = held([P, HP, PACK], F32, "b1_sb")
+        gain_sb = held([P, HP, PACK], F32, "gain_sb")
+        def load_w4_scales(q):
             nc.sync.dma_start(
                 out=w4_sc_raw[32 * q : 32 * q + 4].bitcast(I32),
                 in_=w4_scales[:, 4 * q : 4 * q + 4, :].rearrange("a r c -> r a c").bitcast(I32),
             )
-        w1_raw[1, 0] = load_w1(1, 0)
-        w4_raw = held([P, KP, 2 * H], U8, "w4_raw")
+
         nc.sync.dma_start(out=w4_raw[:].bitcast(I32), in_=w4_words.rearrange("a p c -> p a c").bitcast(I32))
+        nc.sync.dma_start(idx[:], offs)
+        w1_raw[0, 0] = load_w1(0, 0)
+        for q in range(QUADS):
+            nc.sync.dma_start(
+                out=tab_sc[32 * q : 32 * q + 4].bitcast(I32),
+                in_=tab_scales[:, 4 * q : 4 * q + 4, :].rearrange("a r c -> r a c").bitcast(I32),
+            )
+        w1_raw[1, 0] = load_w1(1, 0)
+        load_w4_scales(0)
+        load_w4_scales(1)
         w1_raw[2, 0] = load_w1(2, 0)
-        b1_sb = held([P, HP, PACK], F32, "b1_sb")
-        gain_sb = held([P, HP, PACK], F32, "gain_sb")
-        nc.sync.dma_start(out=b1_sb[:], in_=b1.rearrange("(b p t) -> p b t", p=P, t=PACK))
-        nc.sync.dma_start(out=gain_sb[:], in_=gain.rearrange("(b p t) -> p b t", p=P, t=PACK))
-        nc.sync.dma_start(idx2[:], offs2)
+        load_w4_scales(2)
+        load_w4_scales(3)
         tab_w[0] = load_words(tab_words, 0, "tab_w0")
-        nc.sync.dma_start(idx3[:], offs3)
-        tab_w[1] = load_words(tab_words, 1, "tab_w1")
-        nc.sync.dma_start(idx4[:], offs4)
-        tab_w[2] = load_words(tab_words, 2, "tab_w2")
+        nc.sync.dma_start(out=gain_sb[:], in_=gain.rearrange("(b p t) -> p b t", p=P, t=PACK))
         wgs_first = load_wgs(0, 1, "wgs_first")
+        tab_w[1] = load_words(tab_words, 1, "tab_w1")
+        nc.sync.dma_start(out=b1_sb[:], in_=b1.rearrange("(b p t) -> p b t", p=P, t=PACK))
+        tab_w[2] = load_words(tab_words, 2, "tab_w2")
+        nc.sync.dma_start(idx2[:], offs2)
+        nc.sync.dma_start(idx3[:], offs3)
         pages[0] = load_page(0)
+        nc.sync.dma_start(idx4[:], offs4)
+        w1_raw[0, 1] = load_w1(0, 1)
         comps[0] = load_comp(0)
         wgs_rest = load_wgs(1, PACK, "wgs_rest")
         pages[1] = load_page(1)
-        w1_raw[0, 1] = load_w1(0, 1)
+        w1_raw[1, 1] = load_w1(1, 1)
         pages[2] = load_page(2)
+        w1_raw[2, 1] = load_w1(2, 1)
         comps[1] = load_comp(1)
+        pages[3] = load_page(3)
+        pages[4] = load_page(4)
+        comps[2] = load_comp(2)
+        pages[5] = load_page(5)
+        pages[6] = load_page(6)
+        comps[3] = load_comp(3)
+        pages[7] = load_page(7)
 
-        v_sc = held([P, S], U8, "v_sc")
-        nc.vector.tensor_copy(out=v_sc[:], in_=tab_sc[:].indirect(idx[:]))
-        for a in range(1, KP):
-            nc.gpsimd.dma_start(
-                out=v_sc_low[a - 1][0:SHIFT_ROWS, :].bitcast(I32),
-                in_=v_sc[4 * a : 4 * a + SHIFT_ROWS, :].bitcast(I32),
-            )
-        v_sc_at0 = [v_sc] + v_sc_low
+        v_sc = []
+        for a in range(KP):
+            plane = held([P, S], U8, "v_sc%d" % a)
+            nc.vector.tensor_copy(out=plane[:], in_=tab_sc[:, a, :].indirect(idx[:]))
+            v_sc.append(plane)
 
         w4_sc = held([P, KP * H], U8, "w4_sc")
         nc.vector.tensor_copy(
@@ -157,13 +165,14 @@ def tile_list_duplicate_report_finder_kernel(
             in_=w4_raw[:].bitcast(U16).rearrange("p a (b m t) -> p (a b) t m", t=PACK, m=P),
         )
 
+        rounded_tags = [["round0", "round1", "round0"], ["first_bent", "round1", "round0"]]
         w1_w, w1_sc = {}, {}
 
         def quantize_w1(a, b):
-            rounded = held([P, PACK * PASS], BF16, "w1_bf%d%d" % (a, b), tag="w1_bf", bufs=3)
+            rounded = held([P, PACK * PASS], BF16, "w1_bf%d%d" % (a, b), tag=rounded_tags[b][a])
             nc.scalar.copy(
-                out=rounded[:].rearrange("p (t m j) -> p m j t", t=PACK, j=PACK),
-                in_=w1_raw[a, b][:].rearrange("p j (m t) -> p m j t", t=PACK),
+                out=rounded[:].rearrange("p (t m j) -> p m t j", t=PACK, j=PACK),
+                in_=w1_raw[a, b][:].rearrange("p j (m t) -> p m t j", t=PACK),
             )
             w1_w[a, b] = held([P, PASS], U32, "w1_w%d%d" % (a, b))
             w1_sc[a, b] = held([P, PASS], U8, "w1_sc%d%d" % (a, b))
@@ -172,37 +181,32 @@ def tile_list_duplicate_report_finder_kernel(
         for a in range(KP):
             quantize_w1(a, 0)
 
-        w1_raw[1, 1] = load_w1(1, 1)
-        pages[3] = load_page(3)
-        w1_raw[2, 1] = load_w1(2, 1)
-        pages[4] = load_page(4)
-        comps[2] = load_comp(2)
-        pages[5] = load_page(5)
-
         v_w = []
         for a in range(KP):
             words = held([P, S], U32, "v_w%d" % a)
             nc.vector.tensor_copy(out=words[:], in_=tab_w[a][:].bitcast(U32).indirect(idx[:]))
             v_w.append(words)
 
-        v2_sc = held([P, S2], U8, "v2_sc")
+        v2_sc = held([P, S2], U8, "v2_sc", tag="table2")
         nc.vector.tensor_copy(out=v2_sc[:], in_=tab2_sc[:].indirect(idx2[:]))
 
         tab2_w[0] = load_words(tab2_words, 0, "tab2_w0")
-        pages[6] = load_page(6)
-        comps[3] = load_comp(3)
-        pages[7] = load_page(7)
         tab2_w[1] = load_words(tab2_words, 1, "tab2_w1")
+
+        def pass_order(s):
+            return [2, 0, 1] if s == 1 else [0, 1, 2]
 
         def first_pass(s, a, acc1, acc4):
             b, t = divmod(s, PACK)
+            order = pass_order(s)
+            first, last = a == order[0], a == order[-1]
             nc.tensor.matmul_mx(
                 out=acc1[:],
                 lhsT=w1_w[a, b][:, P * t : P * (t + 1)].bitcast(FP8X4),
                 lhsT_scale=w1_sc[a, b][:, P * t : P * (t + 1)],
                 rhs=v_w[a][:].bitcast(FP8X4),
-                rhs_scale=v_sc[4 * a : P, :],
-                start=(a == 0), stop=(a == KP - 1),
+                rhs_scale=v_sc[a][:],
+                start=first, stop=last,
             )
             c0 = H * a + P * s
             nc.tensor.matmul_mx(
@@ -210,37 +214,35 @@ def tile_list_duplicate_report_finder_kernel(
                 lhsT=w4_w[:, 2 * c0 : 2 * (c0 + P)].bitcast(FP4X4),
                 lhsT_scale=w4_sc[:, c0 : c0 + P],
                 rhs=v_w[a][:].bitcast(FP8X4),
-                rhs_scale=v_sc_at0[a][:],
-                start=(a == 0), stop=(a == KP - 1),
+                rhs_scale=v_sc[a][:],
+                start=first, stop=last,
             )
 
         accs = {}
 
         def open_banks(s):
-            accs[s] = (bank(2 * (s % 4), "acc1_%d" % s), bank(2 * (s % 4) + 1, "acc4_%d" % s))
+            accs[s] = (bank(2 * (s % 2), "acc1_%d" % s), bank(2 * (s % 2) + 1, "acc4_%d" % s))
 
-        for s in range(PACK):
+        for s in range(2):
             open_banks(s)
-        for a in range(KP):
-            for s in range(2):
-                first_pass(s, a, *accs[s])
-        for s in range(2, PACK):
-            for a in range(KP):
+        for s in range(2):
+            for a in pass_order(s):
                 first_pass(s, a, *accs[s])
 
         picked = [held([P, PACK, P_SLOTS], F32, "picked%d" % b) for b in range(HP)]
+        first_bent = held([P, S], F32, "first_bent")
         sums, weights = {}, {}
 
         def features(s):
             b, t = divmod(s, PACK)
             acc1, acc4 = accs[s]
-            bent = held([P, S], F32, "bent%d" % s, tag="bent", bufs=4)
-            nc.scalar.activation(out=bent[:], in_=acc1[:], func=ACT.Tanh, bias=b1_sb[:, b, t : t + 1])
+            bent = first_bent[:] if s == 0 else picked[(s - 1) // PACK][:, (s - 1) % PACK, :]
+            nc.scalar.activation(out=bent, in_=acc1[:], func=ACT.Tanh, bias=b1_sb[:, b, t : t + 1])
             weights[s] = held([P, S], F32, "weight%d" % s, tag="weight", bufs=3)
             rows = wgs_first[:, 0, :] if t == 0 else wgs_rest[:, t - 1, :]
             nc.scalar.activation(out=weights[s][:], in_=rows, func=ACT.Copy, scale=gain_sb[:, b, t : t + 1])
-            sums[s] = held([P, S], F32, "sum%d" % s, tag="sum", bufs=3)
-            nc.vector.tensor_tensor(out=sums[s][:], in0=acc4[:], in1=bent[:], op=ALU.add)
+            sums[s] = held([P, S], F32, "sum%d" % s, tag="sum%d" % (max(s - 1, 0) % 3))
+            nc.vector.tensor_tensor(out=sums[s][:], in0=acc4[:], in1=bent, op=ALU.add)
 
         def put(s):
             nc.vector.tensor_tensor(pages[s][:].indirect(idx3[:]), sums[s][:], weights[s][:], ALU.mult)
@@ -283,9 +285,9 @@ def tile_list_duplicate_report_finder_kernel(
                 links[0] = load_link(0)
                 links[1] = load_link(1)
             if s + 1 < 2 * PACK:
-                if s + 1 >= PACK:
+                if s + 1 >= 2:
                     open_banks(s + 1)
-                    for a in range(KP):
+                    for a in pass_order(s + 1):
                         first_pass(s + 1, a, *accs[s + 1])
                 features(s + 1)
             fetch(s)
@@ -304,7 +306,7 @@ def tile_list_duplicate_report_finder_kernel(
         last_words = held([P, 512], U32, "v2_last", tag="x_bf1")
         gather_v2(1, 1, last_words[:])
 
-        bank_order = [0, 2, 1, 3, 4, 6, 5, 7]
+        bank_order = [4, 5, 6, 7, 0, 2, 1, 3]
         for i in range(S2 // P):
             half, m0 = i // 4, P * (i % 4)
             acc = bank(bank_order[i], "score%d" % i)

from contextlib import ExitStack

import concourse.mybir as mybir

K, H, T, S, T2, P_SLOTS, T3, S2 = 1536, 1024, 2048, 512, 1024, 512, 2048, 1024
FLOPS = 2 * (2 * K * H * S + H * S2 * P_SLOTS)

F32 = mybir.dt.float32
BF16 = mybir.dt.bfloat16
I32 = mybir.dt.int32
U32 = mybir.dt.uint32
U16 = mybir.dt.uint16
U8 = mybir.dt.uint8
FP8X4 = mybir.dt.float8_e4m3fn_x4
FP4X4 = mybir.dt.float4_e2m1fn_x4
ALU = mybir.AluOpType
ACT = mybir.ActivationFunctionType

P = 128
PACK = 4
PASS = P * PACK
KP = K // PASS
HP = H // PASS
QUADS = 4


def tile_list_duplicate_report_finder_kernel(
    tc, tab_words, tab_scales, tab2_words, tab2_scales, w4_words, w4_scales, w1, b1, gain,
    page0, wgs, comp, link, offs, offs2, offs3, offs4, out,
):
    nc = tc.nc
    with ExitStack() as ctx:
        lists = ctx.enter_context(tc.tile_pool(name="lists", bufs=1))
        keep = ctx.enter_context(tc.tile_pool(name="keep", bufs=1))
        psum = ctx.enter_context(tc.psum_pool(name="psum", bufs=1))

        def held(shape, dtype, name, tag=None, bufs=1):
            return keep.tile(shape, dtype, name=name, tag=tag or name, bufs=bufs, align_bytes=64)

        def bank(i, name):
            return psum.tile([P, 512], F32, name=name, tag="bank%d" % i)

        idx = lists.tile([P, S // 16], U16, name="idx")
        idx2 = lists.tile([P, S2 // 16], U16, name="idx2")
        idx3 = lists.tile([P, S // 16], U16, name="idx3")
        idx4 = lists.tile([P, P_SLOTS // 16], U16, name="idx4")

        tab_sc = held([P, KP, T], U8, "tab_sc")
        w4_sc_raw = held([P, KP, H], U8, "w4_sc_raw")
        tab2_sc = held([P, T3], U8, "tab2_sc")
        nc.vector.memset(tab_sc[:, 0:2, :].bitcast(I32), 0)
        nc.gpsimd.memset(tab_sc[:, 2, :].bitcast(I32), 0)
        nc.vector.memset(w4_sc_raw[:].bitcast(I32), 0)
        nc.gpsimd.memset(tab2_sc[:].bitcast(I32), 0)
        for q in range(QUADS):
            nc.gpsimd.dma_start(
                out=tab2_sc[32 * q + 8 : 32 * q + 8 + 4 * HP, :].bitcast(I32),
                in_=tab2_scales[:, 4 * q : 4 * q + 4, :].bitcast(I32),
            )

        def load_w1(a, b):
            raw = held([P, PACK, PASS], F32, "w1_raw%d%d" % (a, b))
            rows = w1[PASS * a : PASS * (a + 1), PASS * b : PASS * (b + 1)]
            nc.sync.dma_start(out=raw[:], in_=rows.rearrange("(p j) c -> p j c", j=PACK))
            return raw

        def load_words(words, a, name):
            tile = held([P, T], I32, name, tag="table%d" % a)
            nc.sync.dma_start(out=tile[:], in_=words[a].rearrange("p t i -> p (t i)").bitcast(I32))
            return tile

        page_rows = page0.rearrange("(b p t) c -> b t p c", p=P, t=PACK)

        def load_page(s):
            tile = held([P, T2], F32, "page%d" % s)
            nc.sync.dma_start(out=tile[:], in_=page_rows[s // PACK, s % PACK])
            return tile

        comp_rows = comp.rearrange("(b p t) j -> b p t j", p=P, t=PACK)

        def load_comp(pair):
            tile = held([P, 2, P_SLOTS], F32, "comp%d" % pair)
            b, t0 = pair // 2, 2 * (pair % 2)
            nc.sync.dma_start(out=tile[:], in_=comp_rows[b, :, t0 : t0 + 2, :])
            return tile

        wgs_rows = wgs.rearrange("(q t) j -> q t j", t=PACK)

        def load_wgs(t0, t1, name):
            tile = held([P, t1 - t0, S], F32, name)
            for q in range(QUADS):
                nc.sync.dma_start(out=tile[32 * q : 32 * (q + 1)], in_=wgs_rows[:, t0:t1, :])
            return tile

        def load_link(half):
            tile = held([P, 4, P_SLOTS], F32, "link%d" % half, tag="w1_raw%d1" % (half + 1))
            rows = link[512 * half : 512 * (half + 1), :]
            nc.sync.dma_start(out=tile[:], in_=rows.rearrange("(i p) j -> p i j", p=P))
            return tile

        w1_raw, tab_w, tab2_w, pages, comps = {}, {}, {}, {}, {}
        w4_raw = held([P, KP, 2 * H], U8, "w4_raw")
        b1_sb = held([P, HP, PACK], F32, "b1_sb")
        gain_sb = held([P, HP, PACK], F32, "gain_sb")
        def load_w4_scales(q):
            nc.sync.dma_start(
                out=w4_sc_raw[32 * q : 32 * q + 4].bitcast(I32),
                in_=w4_scales[:, 4 * q : 4 * q + 4, :].rearrange("a r c -> r a c").bitcast(I32),
            )

        nc.sync.dma_start(out=w4_raw[:].bitcast(I32), in_=w4_words.rearrange("a p c -> p a c").bitcast(I32))
        nc.sync.dma_start(idx[:], offs)
        w1_raw[0, 0] = load_w1(0, 0)
        for q in range(QUADS):
            nc.sync.dma_start(
                out=tab_sc[32 * q : 32 * q + 4].bitcast(I32),
                in_=tab_scales[:, 4 * q : 4 * q + 4, :].rearrange("a r c -> r a c").bitcast(I32),
            )
        w1_raw[1, 0] = load_w1(1, 0)
        load_w4_scales(0)
        load_w4_scales(1)
        w1_raw[2, 0] = load_w1(2, 0)
        load_w4_scales(2)
        load_w4_scales(3)
        tab_w[0] = load_words(tab_words, 0, "tab_w0")
        nc.sync.dma_start(out=gain_sb[:], in_=gain.rearrange("(b p t) -> p b t", p=P, t=PACK))
        wgs_first = load_wgs(0, 1, "wgs_first")
        tab_w[1] = load_words(tab_words, 1, "tab_w1")
        nc.sync.dma_start(out=b1_sb[:], in_=b1.rearrange("(b p t) -> p b t", p=P, t=PACK))
        tab_w[2] = load_words(tab_words, 2, "tab_w2")
        nc.sync.dma_start(idx2[:], offs2)
        nc.sync.dma_start(idx3[:], offs3)
        pages[0] = load_page(0)
        nc.sync.dma_start(idx4[:], offs4)
        w1_raw[0, 1] = load_w1(0, 1)
        comps[0] = load_comp(0)
        wgs_rest = load_wgs(1, PACK, "wgs_rest")
        pages[1] = load_page(1)
        w1_raw[1, 1] = load_w1(1, 1)
        pages[2] = load_page(2)
        w1_raw[2, 1] = load_w1(2, 1)
        comps[1] = load_comp(1)
        pages[3] = load_page(3)
        pages[4] = load_page(4)
        comps[2] = load_comp(2)
        pages[5] = load_page(5)
        pages[6] = load_page(6)
        comps[3] = load_comp(3)
        pages[7] = load_page(7)

        v_sc = []
        for a in range(KP):
            plane = held([P, S], U8, "v_sc%d" % a)
            nc.vector.tensor_copy(out=plane[:], in_=tab_sc[:, a, :].indirect(idx[:]))
            v_sc.append(plane)

        w4_sc = held([P, KP * H], U8, "w4_sc")
        nc.vector.tensor_copy(
            out=w4_sc[:].rearrange("p (g t m) -> p g t m", t=PACK, m=P),
            in_=w4_sc_raw[:].rearrange("p a (b m t) -> p (a b) t m", t=PACK, m=P),
        )
        w4_w = held([P, KP * 2 * H], U8, "w4_w")
        nc.vector.tensor_copy(
            out=w4_w[:].bitcast(U16).rearrange("p (g t m) -> p g t m", t=PACK, m=P),
            in_=w4_raw[:].bitcast(U16).rearrange("p a (b m t) -> p (a b) t m", t=PACK, m=P),
        )

        rounded_tags = [["round0", "round1", "round0"], ["first_bent", "round1", "round0"]]
        w1_w, w1_sc = {}, {}

        def quantize_w1(a, b):
            rounded = held([P, PACK * PASS], BF16, "w1_bf%d%d" % (a, b), tag=rounded_tags[b][a])
            nc.scalar.copy(
                out=rounded[:].rearrange("p (t m j) -> p m t j", t=PACK, j=PACK),
                in_=w1_raw[a, b][:].rearrange("p j (m t) -> p m t j", t=PACK),
            )
            w1_w[a, b] = held([P, PASS], U32, "w1_w%d%d" % (a, b))
            w1_sc[a, b] = held([P, PASS], U8, "w1_sc%d%d" % (a, b))
            nc.vector.quantize_mx(out=w1_w[a, b][:].bitcast(FP8X4), scales=w1_sc[a, b][:], in_=rounded[:])

        for a in range(KP):
            quantize_w1(a, 0)

        v_w = []
        for a in range(KP):
            words = held([P, S], U32, "v_w%d" % a)
            nc.vector.tensor_copy(out=words[:], in_=tab_w[a][:].bitcast(U32).indirect(idx[:]))
            v_w.append(words)

        v2_sc = held([P, S2], U8, "v2_sc", tag="table2")
        nc.vector.tensor_copy(out=v2_sc[:], in_=tab2_sc[:].indirect(idx2[:]))

        tab2_w[0] = load_words(tab2_words, 0, "tab2_w0")
        tab2_w[1] = load_words(tab2_words, 1, "tab2_w1")

        def pass_order(s):
            return [2, 0, 1] if s == 1 else [0, 1, 2]

        def first_pass(s, a, acc1, acc4):
            b, t = divmod(s, PACK)
            order = pass_order(s)
            first, last = a == order[0], a == order[-1]
            nc.tensor.matmul_mx(
                out=acc1[:],
                lhsT=w1_w[a, b][:, P * t : P * (t + 1)].bitcast(FP8X4),
                lhsT_scale=w1_sc[a, b][:, P * t : P * (t + 1)],
                rhs=v_w[a][:].bitcast(FP8X4),
                rhs_scale=v_sc[a][:],
                start=first, stop=last,
            )
            c0 = H * a + P * s
            nc.tensor.matmul_mx(
                out=acc4[:],
                lhsT=w4_w[:, 2 * c0 : 2 * (c0 + P)].bitcast(FP4X4),
                lhsT_scale=w4_sc[:, c0 : c0 + P],
                rhs=v_w[a][:].bitcast(FP8X4),
                rhs_scale=v_sc[a][:],
                start=first, stop=last,
            )

        accs = {}

        def open_banks(s):
            accs[s] = (bank(2 * (s % 2), "acc1_%d" % s), bank(2 * (s % 2) + 1, "acc4_%d" % s))

        for s in range(2):
            open_banks(s)
        for s in range(2):
            for a in pass_order(s):
                first_pass(s, a, *accs[s])

        picked = [held([P, PACK, P_SLOTS], F32, "picked%d" % b) for b in range(HP)]
        first_bent = held([P, S], F32, "first_bent")
        sums, weights = {}, {}

        def features(s):
            b, t = divmod(s, PACK)
            acc1, acc4 = accs[s]
            bent = first_bent[:] if s == 0 else picked[(s - 1) // PACK][:, (s - 1) % PACK, :]
            nc.scalar.activation(out=bent, in_=acc1[:], func=ACT.Tanh, bias=b1_sb[:, b, t : t + 1])
            weights[s] = held([P, S], F32, "weight%d" % s, tag="weight", bufs=3)
            rows = wgs_first[:, 0, :] if t == 0 else wgs_rest[:, t - 1, :]
            nc.scalar.activation(out=weights[s][:], in_=rows, func=ACT.Copy, scale=gain_sb[:, b, t : t + 1])
            sums[s] = held([P, S], F32, "sum%d" % s, tag="sum%d" % (max(s - 1, 0) % 3))
            nc.vector.tensor_tensor(out=sums[s][:], in0=acc4[:], in1=bent, op=ALU.add)

        def put(s):
            nc.vector.tensor_tensor(pages[s][:].indirect(idx3[:]), sums[s][:], weights[s][:], ALU.mult)

        def fetch(s):
            b, t = divmod(s, PACK)
            nc.vector.tensor_tensor(
                picked[b][:, t, :], pages[s][:].indirect(idx4[:]), comps[s // 2][:, s % 2, :], ALU.mult
            )

        x_bf, x_w, x_sc = {}, {}, {}

        def round_x(b):
            x_bf[b] = held([P, PACK * P_SLOTS], BF16, "x_bf%d" % b)
            nc.scalar.copy(
                out=x_bf[b][:].rearrange("p (c i t) -> p c t i", i=4, t=PACK),
                in_=picked[b][:].rearrange("p t (c i) -> p c t i", i=4),
            )

        def quantize_x(b):
            x_w[b] = held([P, P_SLOTS], U32, "x_w%d" % b)
            x_sc[b] = held([P, P_SLOTS], U8, "x_sc%d" % b)
            nc.vector.quantize_mx(out=x_w[b][:].bitcast(FP8X4), scales=x_sc[b][:], in_=x_bf[b][:])

        v2_w = {}

        def gather_v2(a, half, words):
            nc.vector.tensor_copy(
                out=words, in_=tab2_w[a][:].bitcast(U32).indirect(idx2[:, 32 * half : 32 * (half + 1)])
            )
            v2_w[a, half] = words

        links = {}
        features(0)
        for s in range(2 * PACK):
            put(s)
            if s < KP:
                quantize_w1(s, 1)
            if s == KP - 1:
                links[0] = load_link(0)
                links[1] = load_link(1)
            if s + 1 < 2 * PACK:
                if s + 1 >= 2:
                    open_banks(s + 1)
                    for a in pass_order(s + 1):
                        first_pass(s + 1, a, *accs[s + 1])
                features(s + 1)
            fetch(s)
            if s == PACK - 1:
                round_x(0)
            if s == PACK:
                quantize_x(0)
                first_words = held([P, 512], U32, "v2_first")
                gather_v2(0, 0, first_words[:])

        round_x(1)
        late_words = held([P, 2, 512], U32, "v2_late", tag="page7")
        gather_v2(1, 0, late_words[:, 0, :])
        gather_v2(0, 1, late_words[:, 1, :])
        quantize_x(1)
        last_words = held([P, 512], U32, "v2_last", tag="x_bf1")
        gather_v2(1, 1, last_words[:])

        bank_order = [4, 5, 6, 7, 0, 2, 1, 3]
        for i in range(S2 // P):
            half, m0 = i // 4, P * (i % 4)
            acc = bank(bank_order[i], "score%d" % i)
            for a in range(HP):
                nc.tensor.matmul_mx(
                    out=acc[:],
                    lhsT=v2_w[a, half][:, m0 : m0 + P].bitcast(FP8X4),
                    lhsT_scale=v2_sc[8 + 4 * a : P, P * i : P * (i + 1)],
                    rhs=x_w[a][:].bitcast(FP8X4),
                    rhs_scale=x_sc[a][:],
                    start=(a == 0), stop=(a == HP - 1),
                )
            floor = links[half][:, i % 4, :]
            nc.vector.tensor_tensor(out=floor, in0=acc[:], in1=floor, op=ALU.max)
            nc.sync.dma_start(out=out[P * i : P * (i + 1), :], in_=floor)
